import numpy as np
import ml_dtypes


def mxq(x, axis, fmt="e4m3"):
    dtype, down = {"e4m3": (ml_dtypes.float8_e4m3fn, 7), "e5m2": (ml_dtypes.float8_e5m2, 14)}[fmt]
    v = np.moveaxis(np.asarray(x, np.float32).astype(ml_dtypes.bfloat16).astype(np.float64), axis, -1)
    blocks = v.reshape(v.shape[:-1] + (-1, 32))
    amax = np.abs(blocks).max(-1, keepdims=True)
    byte = np.maximum(np.where(amax > 0, np.frexp(amax)[1] - 1 + 127, 0) - down, 1)
    scale = np.exp2(byte - 127.0)
    codes = (blocks / scale).astype(np.float32).astype(dtype).astype(np.float64)
    return np.moveaxis((codes * scale).reshape(v.shape), -1, axis)


WIDE = False


def mx_kscale(k):
    if not WIDE:
        return np.ones(k)
    levels = np.array([10, -10, 5, -5, 0])
    if k % 512:
        return np.exp2(np.random.permutation(np.resize(levels, k // 32))).repeat(32)
    a = np.empty((k // 512, 16))
    for p in range(k // 512):
        a[p, :8] = np.random.permutation(np.resize(levels, 8))
        for g in range(8):
            far = levels[np.abs(levels - a[p, g]) >= 10]
            a[p, g + 8] = far[np.random.randint(len(far))]
    return np.exp2(a.ravel()).repeat(32)


BF16 = ml_dtypes.bfloat16


def bf(x):
    return np.asarray(x, np.float32).astype(BF16)


def f64(x):
    return np.asarray(x).astype(np.float64)


E2M1 = np.array([0.0, 0.5, 1.0, 1.5, 2.0, 3.0, 4.0, 6.0, -0.0, -0.5, -1.0, -1.5, -2.0, -3.0, -4.0, -6.0])


def pack_weight(w, fmt):
    k, n = w.shape
    w = f64(bf(w)).reshape(k // 32, 32, n)
    amax = np.abs(w).max(1)
    if fmt == "e4m3":
        byte = np.frexp(amax)[1] - 1 + 127 - 7
    else:
        mant, ex = np.frexp(amax / 6.0)
        byte = np.where(mant > 0.5, ex, ex - 1) + 127
    byte = np.clip(np.where(amax > 0, byte, 1), 1, 254)
    scaled = (w * np.exp2(127.0 - byte)[:, None, :]).reshape(k, n).astype(np.float32)
    by_word = np.ascontiguousarray(scaled.reshape(k // 512, 128, 4, n).transpose(0, 1, 3, 2))
    if fmt == "e4m3":
        words = by_word.astype(ml_dtypes.float8_e4m3fn).view(np.uint8)
    else:
        c = by_word.astype(ml_dtypes.float4_e2m1fn).view(np.uint8) & 0xF
        words = c[..., 0::2] | (c[..., 1::2] << 4)
    return np.ascontiguousarray(words), np.ascontiguousarray(byte.astype(np.uint8).reshape(k // 512, 16, n))


def unpack_weight(words, scales, fmt):
    g, p, n, _ = words.shape
    if fmt == "e4m3":
        vals = np.ascontiguousarray(words).view(ml_dtypes.float8_e4m3fn).astype(np.float64)
    else:
        nib = np.empty((g, p, n, 4), np.uint8)
        nib[..., 0::2] = words & 0xF
        nib[..., 1::2] = words >> 4
        vals = E2M1[nib]
    vals = vals * np.repeat(np.exp2(scales.astype(np.float64) - 127.0), 8, axis=1)[..., None]
    return vals.transpose(0, 1, 3, 2).reshape(g * 512, n)
def pack4(w):
    words, scales = pack_weight(w, "e2m1")
    return words.reshape(words.shape[0], 128, -1), scales


def unpack4(words, scales):
    return unpack_weight(words.reshape(words.shape[0], 128, -1, 2), scales, "e2m1")


def planes(Y):
    n, m = Y.shape
    b = f64(bf(Y)).reshape(n // 32, 32, m)
    amax = np.abs(b).max(1)
    byte = np.clip(np.where(amax > 0, np.frexp(amax)[1] - 1 + 127 - 7, 1), 1, 254)
    codes = (b * np.exp2(127.0 - byte)[:, None, :]).reshape(n, m).astype(np.float32).astype(ml_dtypes.float8_e4m3fn).view(np.uint8)
    words = codes.reshape(n // 512, 128, 4, m).transpose(0, 1, 3, 2)
    return np.ascontiguousarray(words), np.ascontiguousarray(byte.astype(np.uint8).reshape(n // 512, 16, m))


G, C, D, K, S, P = 4, 1024, 32, 1024, 512, 512

def setup_inputs():
    s = mx_kscale(G * K).reshape(G, K, 1)
    t = mx_kscale(G * C).reshape(G, C, 1)
    design = np.random.randn(G, C, K) * s.reshape(G, 1, K)
    effects = 0.8 * np.random.randn(G, K, S) / np.sqrt(K) / s
    age = np.arange(C) % D
    origin = (np.arange(C) - age) / D
    exposure = np.exp(0.4 * np.random.randn(G, C) - age / D) * t.reshape(G, C)
    diagonal = (origin + age) / (C / D + D)
    near = np.exp(-3.0 * np.abs(diagonal.reshape(C, 1) - np.arange(P).reshape(1, P) / P))
    calendar = (0.5 + near) * np.random.randn(G, C, P) / np.sqrt(C) / t
    effects_words, effects_scales = pack4(effects.reshape(G * K, S))
    calendar_words, calendar_scales = pack4(calendar.reshape(G * C, P))
    return {"design": bf(design), "effects_words": effects_words, "effects_scales": effects_scales,
            "exposure": bf(exposure), "calendar_words": calendar_words, "calendar_scales": calendar_scales,
            "base": bf(0.5 * np.random.randn(G, P)),
            "scenario_scale": bf(np.exp(0.8 * np.random.randn(G, S)))}

def reference(design, effects_words, effects_scales, exposure, calendar_words, calendar_scales, base, scenario_scale):
    E = unpack4(effects_words, effects_scales).reshape(G, K, S)
    A = unpack4(calendar_words, calendar_scales).reshape(G, C, P)
    eta = mxq(f64(design), 2, "e4m3") @ E
    claims = np.exp(eta) * f64(exposure).reshape(G, C, 1)
    net = A.swapaxes(1, 2) @ mxq(claims, 1, "e4m3")
    y = (net + f64(base).reshape(G, P, 1)) * f64(scenario_scale).reshape(G, 1, S)
    Y = y.reshape(G * P, S).T
    words, scales = planes(Y)
    return y, words, scales

@@ -1,0 +1,374 @@
+from contextlib import ExitStack
+
+import concourse.mybir as mybir
+from concourse.masks import make_identity
+
+F32 = mybir.dt.float32
+BF16 = mybir.dt.bfloat16
+I32 = mybir.dt.int32
+U32 = mybir.dt.uint32
+U8 = mybir.dt.uint8
+FP8X4 = mybir.dt.float8_e4m3fn_x4
+FP4X4 = mybir.dt.float4_e2m1fn_x4
+ACT = mybir.ActivationFunctionType
+ALU = mybir.AluOpType
+
+LINES, CELLS, FEATURES, SCENARIOS, PERIODS = 4, 1024, 1024, 512, 512
+P = 128
+FLOPS = 2 * LINES * CELLS * FEATURES * SCENARIOS + 2 * LINES * CELLS * SCENARIOS * PERIODS
+
+GROUPS = 8
+JOBS = 16
+
+
+def tile_runoff_calendar_scenarios_k7_kernel(
+    tc, design, effects_words, effects_scales, exposure, calendar_words, calendar_scales, base,
+    scenario_scale, out_0, out_1, out_2,
+):
+    nc = tc.nc
+    with ExitStack() as ctx:
+        keep = ctx.enter_context(tc.tile_pool(name="keep", bufs=1))
+        stage = ctx.enter_context(tc.tile_pool(name="stage", bufs=1))
+        turn_ps = ctx.enter_context(tc.psum_pool(name="turn_ps", bufs=4))
+        eta_ps = ctx.enter_context(tc.psum_pool(name="eta_ps", bufs=2))
+        net_ps = ctx.enter_context(tc.psum_pool(name="net_ps", bufs=2))
+        ctx.enter_context(tc.manual_schedule())
+
+        ident = keep.tile([P, P], F32, name="ident")
+        make_identity(nc, ident[:])
+
+        e_scales = keep.tile([P, GROUPS, SCENARIOS], U8, name="e_scales", align_bytes=64)
+        a_scales = keep.tile([P, GROUPS, PERIODS], U8, name="a_scales", align_bytes=64)
+        base_rows = keep.tile([P, P], F32, name="base_rows")
+        warm = keep.tile([P, 8], F32, name="warm")
+        warm_out = keep.tile([P, 8], F32, name="warm_out")
+        nc.vector.memset(warm[:], 0.0)
+        nc.vector.memset(e_scales[:].bitcast(I32), 0)
+        nc.scalar.activation(out=warm_out[:], in_=warm[:], func=ACT.Exp)
+        nc.vector.memset(base_rows[:], 0.0)
+        nc.vector.memset(a_scales[:].bitcast(I32), 0)
+
+        rows = {}
+
+        def load_design(n, t0, slots):
+            line, h = divmod(n, 2)
+            tile = keep.tile([P, slots * FEATURES], BF16, name="design_%d_%d" % (n, t0))
+            src = design[line, 512 * h : 512 * (h + 1), :].rearrange("(m t) k -> m (t k)", t=4)
+            nc.sync.dma_start(out=tile[:], in_=src[:, t0 * FEATURES : (t0 + slots) * FEATURES])
+            for s in range(slots):
+                rows[n, t0 + s] = (tile, s)
+
+        def load_words(store, words, name, line0, count):
+            tile = keep.tile([P, 2 * count, 1024], U8, name="%s_%d" % (name, line0), align_bytes=64)
+            src = words[2 * line0 : 2 * (line0 + count)].rearrange("g p b -> p g b")
+            nc.sync.dma_start(out=tile[:].bitcast(I32), in_=src.bitcast(I32))
+            for i in range(count):
+                store[line0 + i] = (tile, 2 * i)
+
+        def load_scales(plane, scales, g0, g1):
+            for quad in range(4):
+                src = scales[g0:g1, 4 * quad : 4 * quad + 4, :].rearrange("g r n -> r g n")
+                nc.sync.dma_start(
+                    out=plane[32 * quad : 32 * quad + 4, g0:g1, :].bitcast(I32),
+                    in_=src.bitcast(I32),
+                )
+
+        e_words, a_words = {}, {}
+        expo = keep.tile([P, GROUPS, 4], BF16, name="expo")
+        base_raw = keep.tile([16, P], BF16, name="base_raw")
+        scen = keep.tile([P, LINES * SCENARIOS], BF16, name="scen")
+
+        for t in range(4):
+            load_design(0, t, 1)
+        load_design(1, 0, 2)
+        load_words(e_words, effects_words, "e_words", 0, 1)
+        load_scales(e_scales, effects_scales, 0, 2)
+        nc.sync.dma_start(out=expo[:], in_=exposure.rearrange("l (h p t) -> p (l h) t", h=2, t=4))
+        load_design(1, 2, 2)
+        nc.sync.dma_start(out=base_raw[:], in_=base.rearrange("l (j p) -> (l j) p", p=P))
+        load_design(2, 0, 2)
+        load_design(2, 2, 2)
+        load_words(a_words, calendar_words, "a_words", 0, 1)
+        load_scales(e_scales, effects_scales, 2, GROUPS)
+        load_scales(a_scales, calendar_scales, 0, GROUPS)
+        load_words(e_words, effects_words, "e_words", 1, 3)
+        nc.sync.dma_start(
+            out=scen[:], in_=scenario_scale.rearrange("l s -> (l s)").partition_broadcast(P)
+        )
+        load_design(3, 0, 2)
+        load_design(3, 2, 2)
+        load_words(a_words, calendar_words, "a_words", 1, 3)
+        for n in range(4, GROUPS):
+            load_design(n, 0, 2)
+            load_design(n, 2, 2)
+
+        base_cols = keep.tile([P, JOBS], F32, name="base_cols")
+        plane_words = keep.tile([P, LINES * PERIODS], U32, name="plane_words", align_bytes=64)
+        plane_scales = keep.tile([P, LINES * PERIODS], U8, name="plane_scales", align_bytes=64)
+
+        turned, grouped, d_codes, d_scales = {}, {}, {}, {}
+        eta, expd, claims, c_codes, c_scales = {}, {}, {}, {}, {}
+        net, y, y_bf, y_turned, y_grouped = {}, {}, {}, {}, {}
+
+        def turn_design(n, t):
+            tile, s = rows[n, t]
+            words = tile[:].bitcast(F32)
+            bank = turn_ps.tile([P, 2, 2, P], F32, name="bank", tag="turn")
+            for g in range(2):
+                for u in range(2):
+                    first = 512 * s + 256 * g + u
+                    nc.tensor.transpose(
+                        bank[:, g, u, :], words[:, first : 512 * s + 256 * (g + 1) : 2], ident[:]
+                    )
+            turned[n, t] = bank
+
+        def group_design(n, t):
+            half, s = divmod(t, 2)
+            if s == 0:
+                grouped[n, half] = stage.tile(
+                    [P, 2048], BF16, name="grouped", tag="grouped", bufs=3, align_bytes=64
+                )
+            dst = grouped[n, half][:].bitcast(F32)[:, 512 * s : 512 * (s + 1)]
+            nc.scalar.copy(
+                out=dst.rearrange("p (g m u) -> p g m u", g=2, u=2),
+                in_=turned[n, t][:].rearrange("p g u m -> p g m u"),
+            )
+
+        def quantize_design(n, t0, slots):
+            half, s = divmod(t0, 2)
+            if s == 0:
+                d_codes[n, half] = stage.tile(
+                    [P, 512], U32, name="d_codes", tag="d_codes", bufs=6, align_bytes=64
+                )
+                d_scales[n, half] = stage.tile(
+                    [P, 512], U8, name="d_scales", tag="d_scales", bufs=6, align_bytes=64
+                )
+            cols = slice(256 * s, 256 * (s + slots))
+            nc.vector.quantize_mx(
+                out=d_codes[n, half][:, cols].bitcast(FP8X4),
+                scales=d_scales[n, half][:, cols],
+                in_=grouped[n, half][:, 1024 * s : 1024 * (s + slots)],
+            )
+
+        def predict(n, c, pool, tag):
+            line = n // 2
+            words, g0 = e_words[line]
+            bank = pool.tile([P, 4, P], F32, name="bank", tag=tag)
+            for t in range(4):
+                half, s = divmod(t, 2)
+                for g in range(2):
+                    cols = slice(256 * s + P * g, 256 * s + P * (g + 1))
+                    nc.tensor.matmul_mx(
+                        out=bank[:, t, :],
+                        lhsT=d_codes[n, half][:, cols].bitcast(FP8X4),
+                        lhsT_scale=d_scales[n, half][:, cols],
+                        rhs=words[:, g0 + g, 256 * c : 256 * (c + 1)].bitcast(FP4X4),
+                        rhs_scale=e_scales[:, 2 * line + g, P * c : P * (c + 1)],
+                        start=(g == 0),
+                        stop=(g == 1),
+                    )
+            eta[n, c] = bank
+
+        def exponential(n, c):
+            tile = stage.tile([P, P, 4], F32, name="expd", tag="expd", bufs=4)
+            nc.scalar.activation(
+                out=tile[:], in_=eta[n, c][:].rearrange("p t s -> p s t"), func=ACT.Exp
+            )
+            expd[n, c] = tile
+
+        def expose(n, c):
+            half, s = divmod(c, 2)
+            if s == 0:
+                claims[n, half] = stage.tile(
+                    [P, 1024], BF16, name="claims", tag="claims", bufs=3, align_bytes=64
+                )
+            nc.vector.tensor_tensor(
+                out=claims[n, half][:, 512 * s : 512 * (s + 1)].rearrange("p (s t) -> p s t", t=4),
+                in0=expd[n, c][:],
+                in1=expo[:, n : n + 1, :].to_broadcast([P, P, 4]),
+                op=ALU.mult,
+            )
+
+        def quantize_claims(n, half):
+            if half == 0:
+                c_codes[n] = keep.tile([P, 512], U32, name="c_codes_%d" % n, align_bytes=64)
+                c_scales[n] = keep.tile([P, 512], U8, name="c_scales_%d" % n, align_bytes=64)
+            cols = slice(256 * half, 256 * (half + 1))
+            nc.vector.quantize_mx(
+                out=c_codes[n][:, cols].bitcast(FP8X4),
+                scales=c_scales[n][:, cols],
+                in_=claims[n, half][:],
+            )
+
+        def aggregate(q, h, pool=None, tag=None):
+            line, j = divmod(q, 4)
+            words, g0 = a_words[line]
+            if h == 0:
+                net[q] = pool.tile([P, SCENARIOS], F32, name="bank", tag=tag)
+            nc.tensor.matmul_mx(
+                out=net[q][:],
+                lhsT=words[:, g0 + h, 256 * j : 256 * (j + 1)].bitcast(FP4X4),
+                lhsT_scale=a_scales[:, 2 * line + h, P * j : P * (j + 1)],
+                rhs=c_codes[2 * line + h][:].bitcast(FP8X4),
+                rhs_scale=c_scales[2 * line + h][:],
+                start=(h == 0),
+                stop=(h == 1),
+            )
+
+        def finish(q):
+            line, j = divmod(q, 4)
+            y[q] = keep.tile([P, SCENARIOS], F32, name="y_%d" % q)
+            nc.vector.scalar_tensor_tensor(
+                out=y[q][:],
+                in0=net[q][:],
+                scalar=base_cols[:, q : q + 1],
+                in1=scen[:, SCENARIOS * line : SCENARIOS * (line + 1)],
+                op0=ALU.add,
+                op1=ALU.mult,
+            )
+            nc.sync.dma_start(out=out_0[line, P * j : P * (j + 1), :], in_=y[q][:])
+
+        def round_y(q, copy):
+            y_bf[q] = stage.tile([P, SCENARIOS], BF16, name="y_bf", tag="y_bf", bufs=6)
+            copy(
+                out=y_bf[q][:].rearrange("d (u p e) -> d u p e", u=2, e=2),
+                in_=y[q][:].rearrange("d (p u e) -> d u p e", u=2, e=2),
+            )
+
+        def turn_y(q0, count):
+            bank = turn_ps.tile([P, 2, 2, P], F32, name="bank", tag="turn")
+            for i in range(count):
+                words = y_bf[q0 + i][:].bitcast(F32)
+                for u in range(2):
+                    nc.tensor.transpose(bank[:, i, u, :], words[:, P * u : P * (u + 1)], ident[:])
+            y_turned[q0] = bank
+
+        def group_y(q0, count, copy):
+            y_grouped[q0] = stage.tile(
+                [P, 1024], BF16, name="y_grouped", tag="y_grouped", bufs=6, align_bytes=64
+            )
+            dst = y_grouped[q0][:].bitcast(F32)[:, 0 : 256 * count]
+            copy(
+                out=dst.rearrange("p (i d u) -> p i d u", i=count, u=2),
+                in_=y_turned[q0][:, 0:count, :, :].rearrange("p i u d -> p i d u"),
+            )
+
+        def quantize_y(q0, count):
+            cols = slice(P * q0, P * (q0 + count))
+            nc.vector.quantize_mx(
+                out=plane_words[:, cols].bitcast(FP8X4),
+                scales=plane_scales[:, cols],
+                in_=y_grouped[q0][:, 0 : 512 * count],
+            )
+
+        def store_words(q0, count):
+            cols = slice(P * q0, P * (q0 + count))
+            dst = out_1[0].rearrange("p m t -> p (m t)").bitcast(I32)
+            nc.sync.dma_start(out=dst[:, cols], in_=plane_words[:, cols].bitcast(I32))
+
+        def store_scales(q0, count, queues):
+            cols = slice(P * q0, P * (q0 + count))
+            for quad in range(4):
+                queues[quad].dma_start(
+                    out=out_2[0, 4 * quad : 4 * quad + 4, cols].bitcast(I32),
+                    in_=plane_scales[32 * quad : 32 * quad + 4, cols].bitcast(I32),
+                )
+
+        for t in range(4):
+            turn_design(0, t)
+            group_design(0, t)
+            quantize_design(0, t, 1)
+
+        for step in range(2 * GROUPS - 2):
+            n, half = divmod(step, 2)
+            q = step - 4
+            if step == 2:
+                base_bank = turn_ps.tile([P, 2, 2, P], F32, name="bank", tag="turn")
+                nc.tensor.transpose(base_bank[:, 0, 0, :], base_rows[:], ident[:])
+                nc.scalar.copy(out=base_cols[:], in_=base_bank[:, 0, 0, 0:JOBS])
+            turn_design(n + 1, 2 * half)
+            turn_design(n + 1, 2 * half + 1)
+            if q >= 3 and q % 2 == 1:
+                turn_y(q - 3, 2)
+            group_design(n + 1, 2 * half)
+            group_design(n + 1, 2 * half + 1)
+            predict(n, 2 * half, eta_ps, "eta")
+            exponential(n, 2 * half)
+            predict(n, 2 * half + 1, eta_ps, "eta")
+            exponential(n, 2 * half + 1)
+            if q >= 0:
+                aggregate(q, 0, net_ps, "net")
+                aggregate(q, 1)
+            quantize_design(n + 1, 2 * half, 2)
+            if step == 0:
+                nc.vector.tensor_copy(out=base_rows[0:16, :], in_=base_raw[:])
+            expose(n, 2 * half)
+            expose(n, 2 * half + 1)
+            if q >= 0:
+                finish(q)
+            quantize_claims(n, half)
+            if q >= 1 and q % 2 == 1:
+                round_y(q - 1, nc.scalar.copy)
+                round_y(q, nc.vector.tensor_copy)
+            if q >= 3 and q % 2 == 1:
+                group_y(q - 3, 2, nc.scalar.copy)
+            if q >= 4 and q % 2 == 0:
+                quantize_y(q - 4, 2)
+                store_words(q - 4, 2)
+
+        last = GROUPS - 1
+        on_scalar, on_vector = nc.scalar.copy, nc.vector.tensor_copy
+        for c in range(4):
+            if c < 2:
+                predict(last, c, eta_ps, "eta")
+            else:
+                predict(last, c, turn_ps, "turn")
+            exponential(last, c)
+        for q in (10, 11):
+            aggregate(q, 0, net_ps, "net")
+            aggregate(q, 1)
+        turn_y(8, 2)
+        group_y(8, 2, on_scalar)
+        expose(last, 0)
+        expose(last, 1)
+        expose(last, 2)
+        quantize_claims(last, 0)
+        expose(last, 3)
+        finish(10)
+        quantize_claims(last, 1)
+        finish(11)
+        round_y(10, on_scalar)
+        round_y(11, on_scalar)
+        aggregate(12, 0, eta_ps, "eta")
+        aggregate(13, 0, eta_ps, "eta")
+        aggregate(14, 0, turn_ps, "turn")
+        aggregate(15, 0, turn_ps, "turn")
+        for q in range(12, 16):
+            aggregate(q, 1)
+        quantize_y(6, 2)
+        store_words(6, 2)
+        store_scales(0, 8, [nc.sync] * 4)
+        turn_y(10, 2)
+        finish(12)
+        round_y(12, on_scalar)
+        group_y(10, 2, on_scalar)
+        finish(13)
+        round_y(13, on_scalar)
+        finish(14)
+        turn_y(12, 2)
+        finish(15)
+        round_y(14, on_vector)
+        round_y(15, on_vector)
+        group_y(12, 2, on_scalar)
+        quantize_y(8, 2)
+        quantize_y(10, 2)
+        store_words(8, 4)
+        turn_y(14, 1)
+        turn_y(15, 1)
+        group_y(14, 1, on_scalar)
+        group_y(15, 1, on_vector)
+        quantize_y(12, 2)
+        quantize_y(14, 1)
+        quantize_y(15, 1)
+        store_words(12, 4)
+        store_scales(8, 8, [nc.sync, nc.sync, nc.scalar, nc.scalar])

@@ -40,9 +40,11 @@ def tile_runoff_calendar_scenarios_k7_kernel(
         e_scales = keep.tile([P, GROUPS, SCENARIOS], U8, name="e_scales", align_bytes=64)
         a_scales = keep.tile([P, GROUPS, PERIODS], U8, name="a_scales", align_bytes=64)
         base_rows = keep.tile([P, P], F32, name="base_rows")
+        expo_rows = keep.tile([P, 512], BF16, name="expo_rows")
         warm = keep.tile([P, 8], F32, name="warm")
         warm_out = keep.tile([P, 8], F32, name="warm_out")
         nc.vector.memset(warm[:], 0.0)
+        nc.vector.memset(expo_rows[:], 0.0)
         nc.vector.memset(e_scales[:].bitcast(I32), 0)
         nc.scalar.activation(out=warm_out[:], in_=warm[:], func=ACT.Exp)
         nc.vector.memset(base_rows[:], 0.0)
@@ -73,32 +75,42 @@ def tile_runoff_calendar_scenarios_k7_kernel(
                     in_=src.bitcast(I32),
                 )
 
+        def load_scenario_scale(line):
+            cols = slice(SCENARIOS * line, SCENARIOS * (line + 1))
+            nc.sync.dma_start(out=scen[:, cols], in_=scenario_scale[line].partition_broadcast(P))
+
         e_words, a_words = {}, {}
         expo = keep.tile([P, GROUPS, 4], BF16, name="expo")
         base_raw = keep.tile([16, P], BF16, name="base_raw")
         scen = keep.tile([P, LINES * SCENARIOS], BF16, name="scen")
 
-        for t in range(4):
-            load_design(0, t, 1)
+        load_design(0, 0, 1)
+        load_design(0, 1, 1)
+        nc.sync.dma_start(
+            out=expo_rows[0:GROUPS, :], in_=exposure.rearrange("l (h c) -> (l h) c", h=2)
+        )
+        nc.sync.dma_start(out=base_raw[:], in_=base.rearrange("l (j p) -> (l j) p", p=P))
+        load_design(0, 2, 1)
+        load_design(0, 3, 1)
         load_design(1, 0, 2)
         load_words(e_words, effects_words, "e_words", 0, 1)
         load_scales(e_scales, effects_scales, 0, 2)
-        nc.sync.dma_start(out=expo[:], in_=exposure.rearrange("l (h p t) -> p (l h) t", h=2, t=4))
         load_design(1, 2, 2)
-        nc.sync.dma_start(out=base_raw[:], in_=base.rearrange("l (j p) -> (l j) p", p=P))
         load_design(2, 0, 2)
-        load_design(2, 2, 2)
-        load_words(a_words, calendar_words, "a_words", 0, 1)
+        load_words(e_words, effects_words, "e_words", 1, 1)
         load_scales(e_scales, effects_scales, 2, GROUPS)
-        load_scales(a_scales, calendar_scales, 0, GROUPS)
-        load_words(e_words, effects_words, "e_words", 1, 3)
-        nc.sync.dma_start(
-            out=scen[:], in_=scenario_scale.rearrange("l s -> (l s)").partition_broadcast(P)
-        )
+        load_design(2, 2, 2)
         load_design(3, 0, 2)
+        load_words(a_words, calendar_words, "a_words", 0, 1)
+        load_scales(a_scales, calendar_scales, 0, GROUPS)
         load_design(3, 2, 2)
+        load_scenario_scale(0)
+        load_design(4, 0, 2)
+        load_words(e_words, effects_words, "e_words", 2, 2)
+        load_design(4, 2, 2)
         load_words(a_words, calendar_words, "a_words", 1, 3)
-        for n in range(4, GROUPS):
+        for n in range(5, GROUPS):
+            load_scenario_scale(n - 4)
             load_design(n, 0, 2)
             load_design(n, 2, 2)
 
@@ -274,18 +286,23 @@ def tile_runoff_calendar_scenarios_k7_kernel(
                     in_=plane_scales[32 * quad : 32 * quad + 4, cols].bitcast(I32),
                 )
 
+        nc.vector.tensor_copy(out=base_rows[0:16, :], in_=base_raw[:])
         for t in range(4):
             turn_design(0, t)
             group_design(0, t)
             quantize_design(0, t, 1)
+        small = turn_ps.tile([P, 2, 2, P], F32, name="bank", tag="turn")
+        for u in range(2):
+            nc.tensor.transpose(small[:, 0, u, :], expo_rows[:].bitcast(F32)[:, u:256:2], ident[:])
+        nc.tensor.transpose(small[:, 1, 0, :], base_rows[:], ident[:])
+        nc.vector.tensor_copy(
+            out=expo[:].bitcast(F32), in_=small[:, 0, :, 0:GROUPS].rearrange("p u n -> p n u")
+        )
+        nc.vector.tensor_copy(out=base_cols[:], in_=small[:, 1, 0, 0:JOBS])
 
         for step in range(2 * GROUPS - 2):
             n, half = divmod(step, 2)
             q = step - 4
-            if step == 2:
-                base_bank = turn_ps.tile([P, 2, 2, P], F32, name="bank", tag="turn")
-                nc.tensor.transpose(base_bank[:, 0, 0, :], base_rows[:], ident[:])
-                nc.scalar.copy(out=base_cols[:], in_=base_bank[:, 0, 0, 0:JOBS])
             turn_design(n + 1, 2 * half)
             turn_design(n + 1, 2 * half + 1)
             if q >= 3 and q % 2 == 1:
@@ -300,8 +317,6 @@ def tile_runoff_calendar_scenarios_k7_kernel(
                 aggregate(q, 0, net_ps, "net")
                 aggregate(q, 1)
             quantize_design(n + 1, 2 * half, 2)
-            if step == 0:
-                nc.vector.tensor_copy(out=base_rows[0:16, :], in_=base_raw[:])
             expose(n, 2 * half)
             expose(n, 2 * half + 1)
             if q >= 0:

@@ -118,9 +118,20 @@ def tile_runoff_calendar_scenarios_k7_kernel(
         plane_words = keep.tile([P, LINES * PERIODS], U32, name="plane_words", align_bytes=64)
         plane_scales = keep.tile([P, LINES * PERIODS], U8, name="plane_scales", align_bytes=64)
 
+        sorted_rows = {}
         turned, grouped, d_codes, d_scales = {}, {}, {}, {}
         eta, expd, claims, c_codes, c_scales = {}, {}, {}, {}, {}
         net, y, y_bf, y_turned, y_grouped = {}, {}, {}, {}, {}
+
+        def sort_design(n, t):
+            tile, s = rows[n, t]
+            src = tile[:].bitcast(F32)[:, 512 * s : 512 * (s + 1)]
+            dst = stage.tile([P, 512], F32, name="sorted_words", tag="sorted_words", bufs=4)
+            nc.vector.tensor_copy(
+                out=dst[:].rearrange("c (g u b i) -> c g b u i", g=2, u=2, i=4),
+                in_=src.rearrange("c (g b i u) -> c g b u i", g=2, u=2, i=4),
+            )
+            sorted_rows[n, t] = dst
 
         def turn_design(n, t):
             tile, s = rows[n, t]
@@ -128,10 +139,12 @@ def tile_runoff_calendar_scenarios_k7_kernel(
             bank = turn_ps.tile([P, 2, 2, P], F32, name="bank", tag="turn")
             for g in range(2):
                 for u in range(2):
-                    first = 512 * s + 256 * g + u
-                    nc.tensor.transpose(
-                        bank[:, g, u, :], words[:, first : 512 * s + 256 * (g + 1) : 2], ident[:]
-                    )
+                    if (n, t) in sorted_rows:
+                        first = 256 * g + P * u
+                        src = sorted_rows[n, t][:, first : first + P]
+                    else:
+                        src = words[:, 512 * s + 256 * g + u : 512 * s + 256 * (g + 1) : 2]
+                    nc.tensor.transpose(bank[:, g, u, :], src, ident[:])
             turned[n, t] = bank
 
         def group_design(n, t):
@@ -300,13 +313,14 @@ def tile_runoff_calendar_scenarios_k7_kernel(
         )
         nc.vector.tensor_copy(out=base_cols[:], in_=small[:, 1, 0, 0:JOBS])
 
+        on_scalar, on_vector = nc.scalar.copy, nc.vector.tensor_copy
         for step in range(2 * GROUPS - 2):
             n, half = divmod(step, 2)
             q = step - 4
             turn_design(n + 1, 2 * half)
             turn_design(n + 1, 2 * half + 1)
-            if q >= 3 and q % 2 == 1:
-                turn_y(q - 3, 2)
+            if q >= 4 and q % 2 == 0:
+                turn_y(q - 4, 2)
             group_design(n + 1, 2 * half)
             group_design(n + 1, 2 * half + 1)
             predict(n, 2 * half, eta_ps, "eta")
@@ -317,73 +331,76 @@ def tile_runoff_calendar_scenarios_k7_kernel(
                 aggregate(q, 0, net_ps, "net")
                 aggregate(q, 1)
             quantize_design(n + 1, 2 * half, 2)
+            ahead = step + 2 + 2
+            count = 1 if ahead < 2 * GROUPS else 0
+            if step == 0:
+                sort_design(1, 2)
+                sort_design(1, 3)
             expose(n, 2 * half)
             expose(n, 2 * half + 1)
             if q >= 0:
                 finish(q)
+            for i in range(count):
+                sort_design(ahead // 2, 2 * (ahead % 2) + i)
             quantize_claims(n, half)
-            if q >= 1 and q % 2 == 1:
-                round_y(q - 1, nc.scalar.copy)
-                round_y(q, nc.vector.tensor_copy)
-            if q >= 3 and q % 2 == 1:
-                group_y(q - 3, 2, nc.scalar.copy)
+            if q >= 1:
+                round_y(q - 1, on_scalar)
             if q >= 4 and q % 2 == 0:
-                quantize_y(q - 4, 2)
-                store_words(q - 4, 2)
+                group_y(q - 4, 2, on_scalar)
+            if q >= 5 and q % 2 == 1:
+                quantize_y(q - 5, 2)
+                store_words(q - 5, 2)
 
         last = GROUPS - 1
-        on_scalar, on_vector = nc.scalar.copy, nc.vector.tensor_copy
         for c in range(4):
             if c < 2:
                 predict(last, c, eta_ps, "eta")
             else:
                 predict(last, c, turn_ps, "turn")
             exponential(last, c)
+        round_y(9, on_scalar)
         for q in (10, 11):
             aggregate(q, 0, net_ps, "net")
             aggregate(q, 1)
+        turn_y(6, 2)
+        group_y(6, 2, on_scalar)
         turn_y(8, 2)
         group_y(8, 2, on_scalar)
+        aggregate(12, 0, eta_ps, "eta")
+        aggregate(13, 0, eta_ps, "eta")
+        aggregate(14, 0, turn_ps, "turn")
+        aggregate(15, 0, turn_ps, "turn")
         expose(last, 0)
         expose(last, 1)
         expose(last, 2)
         quantize_claims(last, 0)
         expose(last, 3)
-        finish(10)
         quantize_claims(last, 1)
-        finish(11)
-        round_y(10, on_scalar)
-        round_y(11, on_scalar)
-        aggregate(12, 0, eta_ps, "eta")
-        aggregate(13, 0, eta_ps, "eta")
-        aggregate(14, 0, turn_ps, "turn")
-        aggregate(15, 0, turn_ps, "turn")
         for q in range(12, 16):
             aggregate(q, 1)
-        quantize_y(6, 2)
-        store_words(6, 2)
-        store_scales(0, 8, [nc.sync] * 4)
-        turn_y(10, 2)
-        finish(12)
-        round_y(12, on_scalar)
+        for q in range(10, 14):
+            finish(q)
+            round_y(q, on_scalar)
+            if q == 11:
+                turn_y(10, 2)
         group_y(10, 2, on_scalar)
-        finish(13)
-        round_y(13, on_scalar)
         finish(14)
         turn_y(12, 2)
         finish(15)
         round_y(14, on_vector)
         round_y(15, on_vector)
         group_y(12, 2, on_scalar)
-        quantize_y(8, 2)
-        quantize_y(10, 2)
-        store_words(8, 4)
         turn_y(14, 1)
         turn_y(15, 1)
         group_y(14, 1, on_scalar)
-        group_y(15, 1, on_vector)
+        group_y(15, 1, on_scalar)
+        quantize_y(6, 2)
+        quantize_y(8, 2)
+        store_words(6, 4)
+        quantize_y(10, 2)
         quantize_y(12, 2)
+        store_words(10, 4)
         quantize_y(14, 1)
         quantize_y(15, 1)
-        store_words(12, 4)
-        store_scales(8, 8, [nc.sync, nc.sync, nc.scalar, nc.scalar])
+        store_words(14, 2)
+        store_scales(0, 16, [nc.sync, nc.sync, nc.scalar, nc.scalar])

@@ -14,11 +14,17 @@ ACT = mybir.ActivationFunctionType
 ALU = mybir.AluOpType
 
 LINES, CELLS, FEATURES, SCENARIOS, PERIODS = 4, 1024, 1024, 512, 512
-P = 128
-FLOPS = 2 * LINES * CELLS * FEATURES * SCENARIOS + 2 * LINES * CELLS * SCENARIOS * PERIODS
+FLOPS = 2 * LINES * CELLS * SCENARIOS * (FEATURES + PERIODS)
 
-GROUPS = 8
-JOBS = 16
+P = 128
+PASS = 4 * P
+SLOT_PAIRS = FEATURES // 2
+GROUPS = LINES * CELLS // PASS
+JOBS = LINES * PERIODS // P
+JOBS_PER_LINE = PERIODS // P
+STEPS = 2 * GROUPS
+JOB_LAG = 4
+SORT_LEAD = 2
 
 
 def tile_runoff_calendar_scenarios_k7_kernel(
@@ -34,214 +40,219 @@ def tile_runoff_calendar_scenarios_k7_kernel(
         net_ps = ctx.enter_context(tc.psum_pool(name="net_ps", bufs=2))
         ctx.enter_context(tc.manual_schedule())
 
+        def bank_of(pool, shape):
+            tag = "turn" if pool is turn_ps else "eta" if pool is eta_ps else "net"
+            return pool.tile(shape, F32, name="bank", tag=tag)
+
         ident = keep.tile([P, P], F32, name="ident")
         make_identity(nc, ident[:])
 
-        e_scales = keep.tile([P, GROUPS, SCENARIOS], U8, name="e_scales", align_bytes=64)
-        a_scales = keep.tile([P, GROUPS, PERIODS], U8, name="a_scales", align_bytes=64)
-        base_rows = keep.tile([P, P], F32, name="base_rows")
-        expo_rows = keep.tile([P, 512], BF16, name="expo_rows")
-        warm = keep.tile([P, 8], F32, name="warm")
-        warm_out = keep.tile([P, 8], F32, name="warm_out")
-        nc.vector.memset(warm[:], 0.0)
-        nc.vector.memset(expo_rows[:], 0.0)
-        nc.vector.memset(e_scales[:].bitcast(I32), 0)
-        nc.scalar.activation(out=warm_out[:], in_=warm[:], func=ACT.Exp)
-        nc.vector.memset(base_rows[:], 0.0)
-        nc.vector.memset(a_scales[:].bitcast(I32), 0)
-
-        rows = {}
+        design_rows, e_words, a_words, e_scales, a_scales = {}, {}, {}, {}, {}
 
         def load_design(n, t0, slots):
             line, h = divmod(n, 2)
             tile = keep.tile([P, slots * FEATURES], BF16, name="design_%d_%d" % (n, t0))
-            src = design[line, 512 * h : 512 * (h + 1), :].rearrange("(m t) k -> m (t k)", t=4)
+            src = design[line, PASS * h : PASS * (h + 1), :].rearrange("(m t) k -> m (t k)", t=4)
             nc.sync.dma_start(out=tile[:], in_=src[:, t0 * FEATURES : (t0 + slots) * FEATURES])
-            for s in range(slots):
-                rows[n, t0 + s] = (tile, s)
+            pairs = tile[:].bitcast(F32)
+            for i in range(slots):
+                design_rows[n, t0 + i] = (pairs, SLOT_PAIRS * i)
 
-        def load_words(store, words, name, line0, count):
-            tile = keep.tile([P, 2 * count, 1024], U8, name="%s_%d" % (name, line0), align_bytes=64)
-            src = words[2 * line0 : 2 * (line0 + count)].rearrange("g p b -> p g b")
+        def load_words(found, words, name, line0, lines):
+            tile = keep.tile([P, 2 * lines, 1024], U8, name="%s_%d" % (name, line0), align_bytes=64)
+            src = words[2 * line0 : 2 * (line0 + lines)].rearrange("g p b -> p g b")
             nc.sync.dma_start(out=tile[:].bitcast(I32), in_=src.bitcast(I32))
-            for i in range(count):
-                store[line0 + i] = (tile, 2 * i)
+            for g in range(2 * lines):
+                found[2 * line0 + g] = tile[:, g, :]
 
-        def load_scales(plane, scales, g0, g1):
+        def scale_tile(found, name, line0, lines):
+            tile = keep.tile([P, 2 * lines, 512], U8, name="%s_%d" % (name, line0), align_bytes=64)
+            nc.vector.memset(tile[:].bitcast(I32), 0)
+            for g in range(2 * lines):
+                found[2 * line0 + g] = tile[:, g, :]
+            return tile
+
+        def load_scales(tile, scales, line0, lines):
             for quad in range(4):
-                src = scales[g0:g1, 4 * quad : 4 * quad + 4, :].rearrange("g r n -> r g n")
+                src = scales[2 * line0 : 2 * (line0 + lines), 4 * quad : 4 * quad + 4, :]
                 nc.sync.dma_start(
-                    out=plane[32 * quad : 32 * quad + 4, g0:g1, :].bitcast(I32),
-                    in_=src.bitcast(I32),
+                    out=tile[32 * quad : 32 * quad + 4].bitcast(I32),
+                    in_=src.rearrange("g r n -> r g n").bitcast(I32),
                 )
 
         def load_scenario_scale(line):
             cols = slice(SCENARIOS * line, SCENARIOS * (line + 1))
             nc.sync.dma_start(out=scen[:, cols], in_=scenario_scale[line].partition_broadcast(P))
 
-        e_words, a_words = {}, {}
+        expo_rows = keep.tile([P, PASS], BF16, name="expo_rows")
+        base_raw = keep.tile([JOBS, P], BF16, name="base_raw")
+        base_rows = keep.tile([P, P], F32, name="base_rows")
         expo = keep.tile([P, GROUPS, 4], BF16, name="expo")
-        base_raw = keep.tile([16, P], BF16, name="base_raw")
+        base_cols = keep.tile([P, JOBS], F32, name="base_cols")
         scen = keep.tile([P, LINES * SCENARIOS], BF16, name="scen")
+
+        nc.vector.memset(expo_rows[:], 0.0)
+        e_first = scale_tile(e_scales, "e_scales", 0, 1)
+        e_rest = scale_tile(e_scales, "e_scales", 1, LINES - 1)
+        a_all = scale_tile(a_scales, "a_scales", 0, LINES)
 
         load_design(0, 0, 1)
         load_design(0, 1, 1)
         nc.sync.dma_start(
             out=expo_rows[0:GROUPS, :], in_=exposure.rearrange("l (h c) -> (l h) c", h=2)
         )
-        nc.sync.dma_start(out=base_raw[:], in_=base.rearrange("l (j p) -> (l j) p", p=P))
+        nc.sync.dma_start(out=base_raw[:], in_=base.rearrange("l (j d) -> (l j) d", d=P))
         load_design(0, 2, 1)
         load_design(0, 3, 1)
-        load_design(1, 0, 2)
         load_words(e_words, effects_words, "e_words", 0, 1)
-        load_scales(e_scales, effects_scales, 0, 2)
+        load_scales(e_first, effects_scales, 0, 1)
+        load_design(1, 0, 2)
         load_design(1, 2, 2)
         load_design(2, 0, 2)
         load_words(e_words, effects_words, "e_words", 1, 1)
-        load_scales(e_scales, effects_scales, 2, GROUPS)
+        load_scales(e_rest, effects_scales, 1, LINES - 1)
         load_design(2, 2, 2)
         load_design(3, 0, 2)
         load_words(a_words, calendar_words, "a_words", 0, 1)
-        load_scales(a_scales, calendar_scales, 0, GROUPS)
+        load_scales(a_all, calendar_scales, 0, LINES)
         load_design(3, 2, 2)
         load_scenario_scale(0)
         load_design(4, 0, 2)
         load_words(e_words, effects_words, "e_words", 2, 2)
         load_design(4, 2, 2)
         load_words(a_words, calendar_words, "a_words", 1, 3)
-        for n in range(5, GROUPS):
-            load_scenario_scale(n - 4)
-            load_design(n, 0, 2)
-            load_design(n, 2, 2)
+        for line in range(1, LINES):
+            load_scenario_scale(line)
+            load_design(4 + line, 0, 2)
+            load_design(4 + line, 2, 2)
 
-        base_cols = keep.tile([P, JOBS], F32, name="base_cols")
+        nc.scalar.activation(out=base_rows[:], in_=ident[:], func=ACT.Copy, scale=0.0)
+
         plane_words = keep.tile([P, LINES * PERIODS], U32, name="plane_words", align_bytes=64)
         plane_scales = keep.tile([P, LINES * PERIODS], U8, name="plane_scales", align_bytes=64)
 
-        sorted_rows = {}
-        turned, grouped, d_codes, d_scales = {}, {}, {}, {}
-        eta, expd, claims, c_codes, c_scales = {}, {}, {}, {}, {}
+        sorted_rows, turned, grouped, d_codes, d_scales = {}, {}, {}, {}, {}
+        exp_eta, claims, c_codes, c_scales = {}, {}, {}, {}
         net, y, y_bf, y_turned, y_grouped = {}, {}, {}, {}, {}
 
-        def sort_design(n, t):
-            tile, s = rows[n, t]
-            src = tile[:].bitcast(F32)[:, 512 * s : 512 * (s + 1)]
-            dst = stage.tile([P, 512], F32, name="sorted_words", tag="sorted_words", bufs=4)
+        def sort_design(n, t0, slots):
+            pairs, first = design_rows[n, t0]
+            src = pairs[:, first : first + SLOT_PAIRS * slots]
+            dst = stage.tile([P, 2 * SLOT_PAIRS], F32, name="sorted", tag="sorted", bufs=3)
             nc.vector.tensor_copy(
-                out=dst[:].rearrange("c (g u b i) -> c g b u i", g=2, u=2, i=4),
-                in_=src.rearrange("c (g b i u) -> c g b u i", g=2, u=2, i=4),
+                out=dst[:, 0 : SLOT_PAIRS * slots].rearrange(
+                    "m (g u b i) -> m g b u i", u=2, b=32, i=4
+                ),
+                in_=src.rearrange("m (g b i u) -> m g b u i", u=2, b=32, i=4),
             )
-            sorted_rows[n, t] = dst
+            for i in range(slots):
+                sorted_rows[n, t0 + i] = dst[:, SLOT_PAIRS * i : SLOT_PAIRS * (i + 1)]
 
         def turn_design(n, t):
-            tile, s = rows[n, t]
-            words = tile[:].bitcast(F32)
-            bank = turn_ps.tile([P, 2, 2, P], F32, name="bank", tag="turn")
+            bank = bank_of(turn_ps, [P, 2, 2, P])
+            pairs, first = design_rows[n, t]
             for g in range(2):
                 for u in range(2):
                     if (n, t) in sorted_rows:
-                        first = 256 * g + P * u
-                        src = sorted_rows[n, t][:, first : first + P]
+                        src = sorted_rows[n, t][:, P * (2 * g + u) : P * (2 * g + u + 1)]
                     else:
-                        src = words[:, 512 * s + 256 * g + u : 512 * s + 256 * (g + 1) : 2]
+                        src = pairs[:, first + 2 * P * g + u : first + 2 * P * (g + 1) : 2]
                     nc.tensor.transpose(bank[:, g, u, :], src, ident[:])
             turned[n, t] = bank
 
         def group_design(n, t):
-            half, s = divmod(t, 2)
-            if s == 0:
+            half, i = divmod(t, 2)
+            if i == 0:
                 grouped[n, half] = stage.tile(
-                    [P, 2048], BF16, name="grouped", tag="grouped", bufs=3, align_bytes=64
+                    [P, 2 * FEATURES], BF16, name="grouped", tag="grouped", bufs=3, align_bytes=64
                 )
-            dst = grouped[n, half][:].bitcast(F32)[:, 512 * s : 512 * (s + 1)]
+            dst = grouped[n, half][:].bitcast(F32)[:, SLOT_PAIRS * i : SLOT_PAIRS * (i + 1)]
             nc.scalar.copy(
                 out=dst.rearrange("p (g m u) -> p g m u", g=2, u=2),
                 in_=turned[n, t][:].rearrange("p g u m -> p g m u"),
             )
 
         def quantize_design(n, t0, slots):
-            half, s = divmod(t0, 2)
-            if s == 0:
+            half, i = divmod(t0, 2)
+            if i == 0:
                 d_codes[n, half] = stage.tile(
-                    [P, 512], U32, name="d_codes", tag="d_codes", bufs=6, align_bytes=64
+                    [P, 4 * P], U32, name="d_codes", tag="d_codes", bufs=6, align_bytes=64
                 )
                 d_scales[n, half] = stage.tile(
-                    [P, 512], U8, name="d_scales", tag="d_scales", bufs=6, align_bytes=64
+                    [P, 4 * P], U8, name="d_scales", tag="d_scales", bufs=6, align_bytes=64
                 )
-            cols = slice(256 * s, 256 * (s + slots))
+            cols = slice(2 * P * i, 2 * P * (i + slots))
             nc.vector.quantize_mx(
                 out=d_codes[n, half][:, cols].bitcast(FP8X4),
                 scales=d_scales[n, half][:, cols],
-                in_=grouped[n, half][:, 1024 * s : 1024 * (s + slots)],
+                in_=grouped[n, half][:, FEATURES * i : FEATURES * (i + slots)],
             )
 
-        def predict(n, c, pool, tag):
+        def predict(n, s, pool):
             line = n // 2
-            words, g0 = e_words[line]
-            bank = pool.tile([P, 4, P], F32, name="bank", tag=tag)
+            bank = bank_of(pool, [P, 4, P])
             for t in range(4):
-                half, s = divmod(t, 2)
+                half, i = divmod(t, 2)
                 for g in range(2):
-                    cols = slice(256 * s + P * g, 256 * s + P * (g + 1))
+                    cols = slice(P * (2 * i + g), P * (2 * i + g + 1))
                     nc.tensor.matmul_mx(
                         out=bank[:, t, :],
                         lhsT=d_codes[n, half][:, cols].bitcast(FP8X4),
                         lhsT_scale=d_scales[n, half][:, cols],
-                        rhs=words[:, g0 + g, 256 * c : 256 * (c + 1)].bitcast(FP4X4),
-                        rhs_scale=e_scales[:, 2 * line + g, P * c : P * (c + 1)],
+                        rhs=e_words[2 * line + g][:, 2 * P * s : 2 * P * (s + 1)].bitcast(FP4X4),
+                        rhs_scale=e_scales[2 * line + g][:, P * s : P * (s + 1)],
                         start=(g == 0),
                         stop=(g == 1),
                     )
-            eta[n, c] = bank
-
-        def exponential(n, c):
-            tile = stage.tile([P, P, 4], F32, name="expd", tag="expd", bufs=4)
+            exp_eta[n, s] = stage.tile([P, P, 4], F32, name="exp_eta", tag="exp_eta", bufs=4)
             nc.scalar.activation(
-                out=tile[:], in_=eta[n, c][:].rearrange("p t s -> p s t"), func=ACT.Exp
+                out=exp_eta[n, s][:], in_=bank[:].rearrange("p t s -> p s t"), func=ACT.Exp
             )
-            expd[n, c] = tile
 
-        def expose(n, c):
-            half, s = divmod(c, 2)
-            if s == 0:
+        def expose(n, s):
+            half, i = divmod(s, 2)
+            if i == 0:
                 claims[n, half] = stage.tile(
-                    [P, 1024], BF16, name="claims", tag="claims", bufs=3, align_bytes=64
+                    [P, 2 * P, 4], BF16, name="claims", tag="claims", bufs=3, align_bytes=64
                 )
             nc.vector.tensor_tensor(
-                out=claims[n, half][:, 512 * s : 512 * (s + 1)].rearrange("p (s t) -> p s t", t=4),
-                in0=expd[n, c][:],
+                out=claims[n, half][:, P * i : P * (i + 1), :],
+                in0=exp_eta[n, s][:],
                 in1=expo[:, n : n + 1, :].to_broadcast([P, P, 4]),
                 op=ALU.mult,
             )
 
         def quantize_claims(n, half):
             if half == 0:
-                c_codes[n] = keep.tile([P, 512], U32, name="c_codes_%d" % n, align_bytes=64)
-                c_scales[n] = keep.tile([P, 512], U8, name="c_scales_%d" % n, align_bytes=64)
-            cols = slice(256 * half, 256 * (half + 1))
+                c_codes[n] = keep.tile([P, SCENARIOS], U32, name="c_codes_%d" % n, align_bytes=64)
+                c_scales[n] = keep.tile([P, SCENARIOS], U8, name="c_scales_%d" % n, align_bytes=64)
+            cols = slice(2 * P * half, 2 * P * (half + 1))
             nc.vector.quantize_mx(
                 out=c_codes[n][:, cols].bitcast(FP8X4),
                 scales=c_scales[n][:, cols],
-                in_=claims[n, half][:],
+                in_=claims[n, half][:].rearrange("p s t -> p (s t)"),
             )
 
-        def aggregate(q, h, pool=None, tag=None):
-            line, j = divmod(q, 4)
-            words, g0 = a_words[line]
-            if h == 0:
-                net[q] = pool.tile([P, SCENARIOS], F32, name="bank", tag=tag)
+        def aggregate_pass(q, h):
+            line, j = divmod(q, JOBS_PER_LINE)
+            n = 2 * line + h
             nc.tensor.matmul_mx(
                 out=net[q][:],
-                lhsT=words[:, g0 + h, 256 * j : 256 * (j + 1)].bitcast(FP4X4),
-                lhsT_scale=a_scales[:, 2 * line + h, P * j : P * (j + 1)],
-                rhs=c_codes[2 * line + h][:].bitcast(FP8X4),
-                rhs_scale=c_scales[2 * line + h][:],
+                lhsT=a_words[n][:, 2 * P * j : 2 * P * (j + 1)].bitcast(FP4X4),
+                lhsT_scale=a_scales[n][:, P * j : P * (j + 1)],
+                rhs=c_codes[n][:].bitcast(FP8X4),
+                rhs_scale=c_scales[n][:],
                 start=(h == 0),
                 stop=(h == 1),
             )
 
+        def aggregate(q):
+            net[q] = bank_of(net_ps, [P, SCENARIOS])
+            aggregate_pass(q, 0)
+            aggregate_pass(q, 1)
+
         def finish(q):
-            line, j = divmod(q, 4)
+            line, j = divmod(q, JOBS_PER_LINE)
             y[q] = keep.tile([P, SCENARIOS], F32, name="y_%d" % q)
             nc.vector.scalar_tensor_tensor(
                 out=y[q][:],
@@ -260,147 +271,138 @@ def tile_runoff_calendar_scenarios_k7_kernel(
                 in_=y[q][:].rearrange("d (p u e) -> d u p e", u=2, e=2),
             )
 
-        def turn_y(q0, count):
-            bank = turn_ps.tile([P, 2, 2, P], F32, name="bank", tag="turn")
-            for i in range(count):
-                words = y_bf[q0 + i][:].bitcast(F32)
+        def turn_y(q0, jobs):
+            bank = bank_of(turn_ps, [P, 2, 2, P])
+            for i in range(jobs):
+                pairs = y_bf[q0 + i][:].bitcast(F32)
                 for u in range(2):
-                    nc.tensor.transpose(bank[:, i, u, :], words[:, P * u : P * (u + 1)], ident[:])
+                    nc.tensor.transpose(bank[:, i, u, :], pairs[:, P * u : P * (u + 1)], ident[:])
             y_turned[q0] = bank
 
-        def group_y(q0, count, copy):
+        def group_y(q0, jobs):
             y_grouped[q0] = stage.tile(
-                [P, 1024], BF16, name="y_grouped", tag="y_grouped", bufs=6, align_bytes=64
+                [P, 2 * SCENARIOS], BF16, name="y_grouped", tag="y_grouped", bufs=6, align_bytes=64
             )
-            dst = y_grouped[q0][:].bitcast(F32)[:, 0 : 256 * count]
-            copy(
-                out=dst.rearrange("p (i d u) -> p i d u", i=count, u=2),
-                in_=y_turned[q0][:, 0:count, :, :].rearrange("p i u d -> p i d u"),
+            dst = y_grouped[q0][:].bitcast(F32)[:, 0 : 2 * P * jobs]
+            nc.scalar.copy(
+                out=dst.rearrange("p (i d u) -> p i d u", i=jobs, u=2),
+                in_=y_turned[q0][:, 0:jobs, :, :].rearrange("p i u d -> p i d u"),
             )
 
-        def quantize_y(q0, count):
-            cols = slice(P * q0, P * (q0 + count))
+        def quantize_y(q0, jobs):
+            cols = slice(P * q0, P * (q0 + jobs))
             nc.vector.quantize_mx(
                 out=plane_words[:, cols].bitcast(FP8X4),
                 scales=plane_scales[:, cols],
-                in_=y_grouped[q0][:, 0 : 512 * count],
+                in_=y_grouped[q0][:, 0 : SCENARIOS * jobs],
             )
 
-        def store_words(q0, count):
-            cols = slice(P * q0, P * (q0 + count))
+        def store_words(q0, jobs):
+            cols = slice(P * q0, P * (q0 + jobs))
             dst = out_1[0].rearrange("p m t -> p (m t)").bitcast(I32)
             nc.sync.dma_start(out=dst[:, cols], in_=plane_words[:, cols].bitcast(I32))
 
-        def store_scales(q0, count, queues):
-            cols = slice(P * q0, P * (q0 + count))
-            for quad in range(4):
-                queues[quad].dma_start(
-                    out=out_2[0, 4 * quad : 4 * quad + 4, cols].bitcast(I32),
-                    in_=plane_scales[32 * quad : 32 * quad + 4, cols].bitcast(I32),
-                )
-
-        nc.vector.tensor_copy(out=base_rows[0:16, :], in_=base_raw[:])
+        nc.vector.tensor_copy(out=base_rows[0:JOBS, :], in_=base_raw[:])
         for t in range(4):
             turn_design(0, t)
             group_design(0, t)
             quantize_design(0, t, 1)
-        small = turn_ps.tile([P, 2, 2, P], F32, name="bank", tag="turn")
+        small = bank_of(turn_ps, [P, 2, 2, P])
         for u in range(2):
-            nc.tensor.transpose(small[:, 0, u, :], expo_rows[:].bitcast(F32)[:, u:256:2], ident[:])
+            pairs = expo_rows[:].bitcast(F32)
+            nc.tensor.transpose(small[:, 0, u, :], pairs[:, u : 2 * P : 2], ident[:])
         nc.tensor.transpose(small[:, 1, 0, :], base_rows[:], ident[:])
         nc.vector.tensor_copy(
             out=expo[:].bitcast(F32), in_=small[:, 0, :, 0:GROUPS].rearrange("p u n -> p n u")
         )
         nc.vector.tensor_copy(out=base_cols[:], in_=small[:, 1, 0, 0:JOBS])
+        predict(0, 0, eta_ps)
+        predict(0, 1, eta_ps)
+        sort_design(1, 0, 2)
+        sort_design(1, 2, 2)
+        turn_design(1, 0)
+        turn_design(1, 1)
+        group_design(1, 0)
+        group_design(1, 1)
+        expose(0, 0)
+        expose(0, 1)
+        sort_design(2, 0, 1)
+        quantize_claims(0, 0)
+        quantize_design(1, 0, 2)
 
-        on_scalar, on_vector = nc.scalar.copy, nc.vector.tensor_copy
-        for step in range(2 * GROUPS - 2):
+        for step in range(1, STEPS - 2):
             n, half = divmod(step, 2)
-            q = step - 4
+            q = step - JOB_LAG
             turn_design(n + 1, 2 * half)
             turn_design(n + 1, 2 * half + 1)
-            if q >= 4 and q % 2 == 0:
+            if q >= 4 and half == 0:
                 turn_y(q - 4, 2)
             group_design(n + 1, 2 * half)
             group_design(n + 1, 2 * half + 1)
-            predict(n, 2 * half, eta_ps, "eta")
-            exponential(n, 2 * half)
-            predict(n, 2 * half + 1, eta_ps, "eta")
-            exponential(n, 2 * half + 1)
+            predict(n, 2 * half, eta_ps)
+            predict(n, 2 * half + 1, eta_ps)
             if q >= 0:
-                aggregate(q, 0, net_ps, "net")
-                aggregate(q, 1)
+                aggregate(q)
             quantize_design(n + 1, 2 * half, 2)
-            ahead = step + 2 + 2
-            count = 1 if ahead < 2 * GROUPS else 0
-            if step == 0:
-                sort_design(1, 2)
-                sort_design(1, 3)
             expose(n, 2 * half)
             expose(n, 2 * half + 1)
             if q >= 0:
                 finish(q)
-            for i in range(count):
-                sort_design(ahead // 2, 2 * (ahead % 2) + i)
+            if step + SORT_LEAD < STEPS - 2:
+                n_later, half_later = divmod(step + SORT_LEAD, 2)
+                sort_design(n_later + 1, 2 * half_later, 1)
             quantize_claims(n, half)
             if q >= 1:
-                round_y(q - 1, on_scalar)
-            if q >= 4 and q % 2 == 0:
-                group_y(q - 4, 2, on_scalar)
-            if q >= 5 and q % 2 == 1:
+                round_y(q - 1, nc.scalar.copy)
+            if q >= 4 and half == 0:
+                group_y(q - 4, 2)
+            if q >= 5 and half == 1:
                 quantize_y(q - 5, 2)
                 store_words(q - 5, 2)
 
         last = GROUPS - 1
-        for c in range(4):
-            if c < 2:
-                predict(last, c, eta_ps, "eta")
-            else:
-                predict(last, c, turn_ps, "turn")
-            exponential(last, c)
-        round_y(9, on_scalar)
-        for q in (10, 11):
-            aggregate(q, 0, net_ps, "net")
-            aggregate(q, 1)
-        turn_y(6, 2)
-        group_y(6, 2, on_scalar)
-        turn_y(8, 2)
-        group_y(8, 2, on_scalar)
-        aggregate(12, 0, eta_ps, "eta")
-        aggregate(13, 0, eta_ps, "eta")
-        aggregate(14, 0, turn_ps, "turn")
-        aggregate(15, 0, turn_ps, "turn")
-        expose(last, 0)
-        expose(last, 1)
-        expose(last, 2)
+        waiting = STEPS - 2 - JOB_LAG
+        last_line = range(JOBS - JOBS_PER_LINE, JOBS)
+        for s, pool in enumerate((eta_ps, eta_ps, turn_ps, turn_ps)):
+            predict(last, s, pool)
+        round_y(waiting - 1, nc.scalar.copy)
+        aggregate(waiting)
+        aggregate(waiting + 1)
+        for q0 in (waiting - 4, waiting - 2):
+            turn_y(q0, 2)
+            group_y(q0, 2)
+        for q, pool in zip(last_line, (eta_ps, eta_ps, turn_ps, turn_ps)):
+            net[q] = bank_of(pool, [P, SCENARIOS])
+            aggregate_pass(q, 0)
+        for s in range(3):
+            expose(last, s)
         quantize_claims(last, 0)
         expose(last, 3)
         quantize_claims(last, 1)
-        for q in range(12, 16):
-            aggregate(q, 1)
-        for q in range(10, 14):
+        for q in last_line:
+            aggregate_pass(q, 1)
+        for q in range(waiting, JOBS - 2):
             finish(q)
-            round_y(q, on_scalar)
-            if q == 11:
-                turn_y(10, 2)
-        group_y(10, 2, on_scalar)
-        finish(14)
-        turn_y(12, 2)
-        finish(15)
-        round_y(14, on_vector)
-        round_y(15, on_vector)
-        group_y(12, 2, on_scalar)
-        turn_y(14, 1)
-        turn_y(15, 1)
-        group_y(14, 1, on_scalar)
-        group_y(15, 1, on_scalar)
-        quantize_y(6, 2)
-        quantize_y(8, 2)
-        store_words(6, 4)
-        quantize_y(10, 2)
-        quantize_y(12, 2)
-        store_words(10, 4)
-        quantize_y(14, 1)
-        quantize_y(15, 1)
-        store_words(14, 2)
-        store_scales(0, 16, [nc.sync, nc.sync, nc.scalar, nc.scalar])
+            round_y(q, nc.scalar.copy)
+        turn_y(waiting, 2)
+        group_y(waiting, 2)
+        finish(JOBS - 2)
+        finish(JOBS - 1)
+        turn_y(waiting + 2, 2)
+        group_y(waiting + 2, 2)
+        for q in (JOBS - 2, JOBS - 1):
+            round_y(q, nc.vector.tensor_copy)
+            turn_y(q, 1)
+            group_y(q, 1)
+        for q0 in (waiting - 4, waiting):
+            quantize_y(q0, 2)
+            quantize_y(q0 + 2, 2)
+            store_words(q0, 4)
+        quantize_y(JOBS - 2, 1)
+        quantize_y(JOBS - 1, 1)
+        store_words(JOBS - 2, 2)
+        for quad, queue in enumerate((nc.sync, nc.sync, nc.scalar, nc.scalar)):
+            queue.dma_start(
+                out=out_2[0, 4 * quad : 4 * quad + 4, :].bitcast(I32),
+                in_=plane_scales[32 * quad : 32 * quad + 4, :].bitcast(I32),
+            )

from contextlib import ExitStack

import concourse.mybir as mybir
from concourse.masks import make_identity

F32 = mybir.dt.float32
BF16 = mybir.dt.bfloat16
I32 = mybir.dt.int32
U32 = mybir.dt.uint32
U8 = mybir.dt.uint8
FP8X4 = mybir.dt.float8_e4m3fn_x4
FP4X4 = mybir.dt.float4_e2m1fn_x4
ACT = mybir.ActivationFunctionType
ALU = mybir.AluOpType

LINES, CELLS, FEATURES, SCENARIOS, PERIODS = 4, 1024, 1024, 512, 512
FLOPS = 2 * LINES * CELLS * SCENARIOS * (FEATURES + PERIODS)

P = 128
PASS = 4 * P
SLOT_PAIRS = FEATURES // 2
GROUPS = LINES * CELLS // PASS
JOBS = LINES * PERIODS // P
JOBS_PER_LINE = PERIODS // P
STEPS = 2 * GROUPS
JOB_LAG = 4
SORT_LEAD = 2


def tile_runoff_calendar_scenarios_k7_kernel(
    tc, design, effects_words, effects_scales, exposure, calendar_words, calendar_scales, base,
    scenario_scale, out_0, out_1, out_2,
):
    nc = tc.nc
    with ExitStack() as ctx:
        keep = ctx.enter_context(tc.tile_pool(name="keep", bufs=1))
        stage = ctx.enter_context(tc.tile_pool(name="stage", bufs=1))
        turn_ps = ctx.enter_context(tc.psum_pool(name="turn_ps", bufs=4))
        eta_ps = ctx.enter_context(tc.psum_pool(name="eta_ps", bufs=2))
        net_ps = ctx.enter_context(tc.psum_pool(name="net_ps", bufs=2))
        ctx.enter_context(tc.manual_schedule())

        def bank_of(pool, shape):
            tag = "turn" if pool is turn_ps else "eta" if pool is eta_ps else "net"
            return pool.tile(shape, F32, name="bank", tag=tag)

        ident = keep.tile([P, P], F32, name="ident")
        make_identity(nc, ident[:])

        design_rows, e_words, a_words, e_scales, a_scales = {}, {}, {}, {}, {}

        def load_design(n, t0, slots):
            line, h = divmod(n, 2)
            tile = keep.tile([P, slots * FEATURES], BF16, name="design_%d_%d" % (n, t0))
            src = design[line, PASS * h : PASS * (h + 1), :].rearrange("(m t) k -> m (t k)", t=4)
            nc.sync.dma_start(out=tile[:], in_=src[:, t0 * FEATURES : (t0 + slots) * FEATURES])
            pairs = tile[:].bitcast(F32)
            for i in range(slots):
                design_rows[n, t0 + i] = (pairs, SLOT_PAIRS * i)

        def load_words(found, words, name, line0, lines):
            tile = keep.tile([P, 2 * lines, 1024], U8, name="%s_%d" % (name, line0), align_bytes=64)
            src = words[2 * line0 : 2 * (line0 + lines)].rearrange("g p b -> p g b")
            nc.sync.dma_start(out=tile[:].bitcast(I32), in_=src.bitcast(I32))
            for g in range(2 * lines):
                found[2 * line0 + g] = tile[:, g, :]

        def scale_tile(found, name, line0, lines):
            tile = keep.tile([P, 2 * lines, 512], U8, name="%s_%d" % (name, line0), align_bytes=64)
            nc.vector.memset(tile[:].bitcast(I32), 0)
            for g in range(2 * lines):
                found[2 * line0 + g] = tile[:, g, :]
            return tile

        def load_scales(tile, scales, line0, lines):
            for quad in range(4):
                src = scales[2 * line0 : 2 * (line0 + lines), 4 * quad : 4 * quad + 4, :]
                nc.sync.dma_start(
                    out=tile[32 * quad : 32 * quad + 4].bitcast(I32),
                    in_=src.rearrange("g r n -> r g n").bitcast(I32),
                )

        def load_scenario_scale(line):
            cols = slice(SCENARIOS * line, SCENARIOS * (line + 1))
            nc.sync.dma_start(out=scen[:, cols], in_=scenario_scale[line].partition_broadcast(P))

        expo_rows = keep.tile([P, PASS], BF16, name="expo_rows")
        base_raw = keep.tile([JOBS, P], BF16, name="base_raw")
        base_rows = keep.tile([P, P], F32, name="base_rows")
        expo = keep.tile([P, GROUPS, 4], BF16, name="expo")
        base_cols = keep.tile([P, JOBS], F32, name="base_cols")
        scen = keep.tile([P, LINES * SCENARIOS], BF16, name="scen")

        nc.vector.memset(expo_rows[:], 0.0)
        e_first = scale_tile(e_scales, "e_scales", 0, 1)
        e_rest = scale_tile(e_scales, "e_scales", 1, LINES - 1)
        a_all = scale_tile(a_scales, "a_scales", 0, LINES)

        load_design(0, 0, 1)
        load_design(0, 1, 1)
        nc.sync.dma_start(
            out=expo_rows[0:GROUPS, :], in_=exposure.rearrange("l (h c) -> (l h) c", h=2)
        )
        nc.sync.dma_start(out=base_raw[:], in_=base.rearrange("l (j d) -> (l j) d", d=P))
        load_design(0, 2, 1)
        load_design(0, 3, 1)
        load_words(e_words, effects_words, "e_words", 0, 1)
        load_scales(e_first, effects_scales, 0, 1)
        load_design(1, 0, 2)
        load_design(1, 2, 2)
        load_design(2, 0, 2)
        load_words(e_words, effects_words, "e_words", 1, 1)
        load_scales(e_rest, effects_scales, 1, LINES - 1)
        load_design(2, 2, 2)
        load_design(3, 0, 2)
        load_words(a_words, calendar_words, "a_words", 0, 1)
        load_scales(a_all, calendar_scales, 0, LINES)
        load_design(3, 2, 2)
        load_scenario_scale(0)
        load_design(4, 0, 2)
        load_words(e_words, effects_words, "e_words", 2, 2)
        load_design(4, 2, 2)
        load_words(a_words, calendar_words, "a_words", 1, 3)
        for line in range(1, LINES):
            load_scenario_scale(line)
            load_design(4 + line, 0, 2)
            load_design(4 + line, 2, 2)

        nc.scalar.activation(out=base_rows[:], in_=ident[:], func=ACT.Copy, scale=0.0)

        plane_words = keep.tile([P, LINES * PERIODS], U32, name="plane_words", align_bytes=64)
        plane_scales = keep.tile([P, LINES * PERIODS], U8, name="plane_scales", align_bytes=64)

        sorted_rows, turned, grouped, d_codes, d_scales = {}, {}, {}, {}, {}
        exp_eta, claims, c_codes, c_scales = {}, {}, {}, {}
        net, y, y_bf, y_turned, y_grouped = {}, {}, {}, {}, {}

        def sort_design(n, t0, slots):
            pairs, first = design_rows[n, t0]
            src = pairs[:, first : first + SLOT_PAIRS * slots]
            dst = stage.tile([P, 2 * SLOT_PAIRS], F32, name="sorted", tag="sorted", bufs=3)
            nc.vector.tensor_copy(
                out=dst[:, 0 : SLOT_PAIRS * slots].rearrange(
                    "m (g u b i) -> m g b u i", u=2, b=32, i=4
                ),
                in_=src.rearrange("m (g b i u) -> m g b u i", u=2, b=32, i=4),
            )
            for i in range(slots):
                sorted_rows[n, t0 + i] = dst[:, SLOT_PAIRS * i : SLOT_PAIRS * (i + 1)]

        def turn_design(n, t):
            bank = bank_of(turn_ps, [P, 2, 2, P])
            pairs, first = design_rows[n, t]
            for g in range(2):
                for u in range(2):
                    if (n, t) in sorted_rows:
                        src = sorted_rows[n, t][:, P * (2 * g + u) : P * (2 * g + u + 1)]
                    else:
                        src = pairs[:, first + 2 * P * g + u : first + 2 * P * (g + 1) : 2]
                    nc.tensor.transpose(bank[:, g, u, :], src, ident[:])
            turned[n, t] = bank

        def group_design(n, t):
            half, i = divmod(t, 2)
            if i == 0:
                grouped[n, half] = stage.tile(
                    [P, 2 * FEATURES], BF16, name="grouped", tag="grouped", bufs=3, align_bytes=64
                )
            dst = grouped[n, half][:].bitcast(F32)[:, SLOT_PAIRS * i : SLOT_PAIRS * (i + 1)]
            nc.scalar.copy(
                out=dst.rearrange("p (g m u) -> p g m u", g=2, u=2),
                in_=turned[n, t][:].rearrange("p g u m -> p g m u"),
            )

        def quantize_design(n, t0, slots):
            half, i = divmod(t0, 2)
            if i == 0:
                d_codes[n, half] = stage.tile(
                    [P, 4 * P], U32, name="d_codes", tag="d_codes", bufs=6, align_bytes=64
                )
                d_scales[n, half] = stage.tile(
                    [P, 4 * P], U8, name="d_scales", tag="d_scales", bufs=6, align_bytes=64
                )
            cols = slice(2 * P * i, 2 * P * (i + slots))
            nc.vector.quantize_mx(
                out=d_codes[n, half][:, cols].bitcast(FP8X4),
                scales=d_scales[n, half][:, cols],
                in_=grouped[n, half][:, FEATURES * i : FEATURES * (i + slots)],
            )

        def predict(n, s, pool):
            line = n // 2
            bank = bank_of(pool, [P, 4, P])
            for t in range(4):
                half, i = divmod(t, 2)
                for g in range(2):
                    cols = slice(P * (2 * i + g), P * (2 * i + g + 1))
                    nc.tensor.matmul_mx(
                        out=bank[:, t, :],
                        lhsT=d_codes[n, half][:, cols].bitcast(FP8X4),
                        lhsT_scale=d_scales[n, half][:, cols],
                        rhs=e_words[2 * line + g][:, 2 * P * s : 2 * P * (s + 1)].bitcast(FP4X4),
                        rhs_scale=e_scales[2 * line + g][:, P * s : P * (s + 1)],
                        start=(g == 0),
                        stop=(g == 1),
                    )
            exp_eta[n, s] = stage.tile([P, P, 4], F32, name="exp_eta", tag="exp_eta", bufs=4)
            nc.scalar.activation(
                out=exp_eta[n, s][:], in_=bank[:].rearrange("p t s -> p s t"), func=ACT.Exp
            )

        def expose(n, s):
            half, i = divmod(s, 2)
            if i == 0:
                claims[n, half] = stage.tile(
                    [P, 2 * P, 4], BF16, name="claims", tag="claims", bufs=3, align_bytes=64
                )
            nc.vector.tensor_tensor(
                out=claims[n, half][:, P * i : P * (i + 1), :],
                in0=exp_eta[n, s][:],
                in1=expo[:, n : n + 1, :].to_broadcast([P, P, 4]),
                op=ALU.mult,
            )

        def quantize_claims(n, half):
            if half == 0:
                c_codes[n] = keep.tile([P, SCENARIOS], U32, name="c_codes_%d" % n, align_bytes=64)
                c_scales[n] = keep.tile([P, SCENARIOS], U8, name="c_scales_%d" % n, align_bytes=64)
            cols = slice(2 * P * half, 2 * P * (half + 1))
            nc.vector.quantize_mx(
                out=c_codes[n][:, cols].bitcast(FP8X4),
                scales=c_scales[n][:, cols],
                in_=claims[n, half][:].rearrange("p s t -> p (s t)"),
            )

        def aggregate_pass(q, h):
            line, j = divmod(q, JOBS_PER_LINE)
            n = 2 * line + h
            nc.tensor.matmul_mx(
                out=net[q][:],
                lhsT=a_words[n][:, 2 * P * j : 2 * P * (j + 1)].bitcast(FP4X4),
                lhsT_scale=a_scales[n][:, P * j : P * (j + 1)],
                rhs=c_codes[n][:].bitcast(FP8X4),
                rhs_scale=c_scales[n][:],
                start=(h == 0),
                stop=(h == 1),
            )

        def aggregate(q):
            net[q] = bank_of(net_ps, [P, SCENARIOS])
            aggregate_pass(q, 0)
            aggregate_pass(q, 1)

        def finish(q):
            line, j = divmod(q, JOBS_PER_LINE)
            y[q] = keep.tile([P, SCENARIOS], F32, name="y_%d" % q)
            nc.vector.scalar_tensor_tensor(
                out=y[q][:],
                in0=net[q][:],
                scalar=base_cols[:, q : q + 1],
                in1=scen[:, SCENARIOS * line : SCENARIOS * (line + 1)],
                op0=ALU.add,
                op1=ALU.mult,
            )
            nc.sync.dma_start(out=out_0[line, P * j : P * (j + 1), :], in_=y[q][:])

        def round_y(q, copy):
            y_bf[q] = stage.tile([P, SCENARIOS], BF16, name="y_bf", tag="y_bf", bufs=6)
            copy(
                out=y_bf[q][:].rearrange("d (u p e) -> d u p e", u=2, e=2),
                in_=y[q][:].rearrange("d (p u e) -> d u p e", u=2, e=2),
            )

        def turn_y(q0, jobs):
            bank = bank_of(turn_ps, [P, 2, 2, P])
            for i in range(jobs):
                pairs = y_bf[q0 + i][:].bitcast(F32)
                for u in range(2):
                    nc.tensor.transpose(bank[:, i, u, :], pairs[:, P * u : P * (u + 1)], ident[:])
            y_turned[q0] = bank

        def group_y(q0, jobs):
            y_grouped[q0] = stage.tile(
                [P, 2 * SCENARIOS], BF16, name="y_grouped", tag="y_grouped", bufs=6, align_bytes=64
            )
            dst = y_grouped[q0][:].bitcast(F32)[:, 0 : 2 * P * jobs]
            nc.scalar.copy(
                out=dst.rearrange("p (i d u) -> p i d u", i=jobs, u=2),
                in_=y_turned[q0][:, 0:jobs, :, :].rearrange("p i u d -> p i d u"),
            )

        def quantize_y(q0, jobs):
            cols = slice(P * q0, P * (q0 + jobs))
            nc.vector.quantize_mx(
                out=plane_words[:, cols].bitcast(FP8X4),
                scales=plane_scales[:, cols],
                in_=y_grouped[q0][:, 0 : SCENARIOS * jobs],
            )

        def store_words(q0, jobs):
            cols = slice(P * q0, P * (q0 + jobs))
            dst = out_1[0].rearrange("p m t -> p (m t)").bitcast(I32)
            nc.sync.dma_start(out=dst[:, cols], in_=plane_words[:, cols].bitcast(I32))

        nc.vector.tensor_copy(out=base_rows[0:JOBS, :], in_=base_raw[:])
        for t in range(4):
            turn_design(0, t)
            group_design(0, t)
            quantize_design(0, t, 1)
        small = bank_of(turn_ps, [P, 2, 2, P])
        for u in range(2):
            pairs = expo_rows[:].bitcast(F32)
            nc.tensor.transpose(small[:, 0, u, :], pairs[:, u : 2 * P : 2], ident[:])
        nc.tensor.transpose(small[:, 1, 0, :], base_rows[:], ident[:])
        nc.vector.tensor_copy(
            out=expo[:].bitcast(F32), in_=small[:, 0, :, 0:GROUPS].rearrange("p u n -> p n u")
        )
        nc.vector.tensor_copy(out=base_cols[:], in_=small[:, 1, 0, 0:JOBS])
        predict(0, 0, eta_ps)
        predict(0, 1, eta_ps)
        sort_design(1, 0, 2)
        sort_design(1, 2, 2)
        turn_design(1, 0)
        turn_design(1, 1)
        group_design(1, 0)
        group_design(1, 1)
        expose(0, 0)
        expose(0, 1)
        sort_design(2, 0, 1)
        quantize_claims(0, 0)
        quantize_design(1, 0, 2)

        for step in range(1, STEPS - 2):
            n, half = divmod(step, 2)
            q = step - JOB_LAG
            turn_design(n + 1, 2 * half)
            turn_design(n + 1, 2 * half + 1)
            if q >= 4 and half == 0:
                turn_y(q - 4, 2)
            group_design(n + 1, 2 * half)
            group_design(n + 1, 2 * half + 1)
            predict(n, 2 * half, eta_ps)
            predict(n, 2 * half + 1, eta_ps)
            if q >= 0:
                aggregate(q)
            quantize_design(n + 1, 2 * half, 2)
            expose(n, 2 * half)
            expose(n, 2 * half + 1)
            if q >= 0:
                finish(q)
            if step + SORT_LEAD < STEPS - 2:
                n_later, half_later = divmod(step + SORT_LEAD, 2)
                sort_design(n_later + 1, 2 * half_later, 1)
            quantize_claims(n, half)
            if q >= 1:
                round_y(q - 1, nc.scalar.copy)
            if q >= 4 and half == 0:
                group_y(q - 4, 2)
            if q >= 5 and half == 1:
                quantize_y(q - 5, 2)
                store_words(q - 5, 2)

        last = GROUPS - 1
        waiting = STEPS - 2 - JOB_LAG
        last_line = range(JOBS - JOBS_PER_LINE, JOBS)
        for s, pool in enumerate((eta_ps, eta_ps, turn_ps, turn_ps)):
            predict(last, s, pool)
        round_y(waiting - 1, nc.scalar.copy)
        aggregate(waiting)
        aggregate(waiting + 1)
        for q0 in (waiting - 4, waiting - 2):
            turn_y(q0, 2)
            group_y(q0, 2)
        for q, pool in zip(last_line, (eta_ps, eta_ps, turn_ps, turn_ps)):
            net[q] = bank_of(pool, [P, SCENARIOS])
            aggregate_pass(q, 0)
        for s in range(3):
            expose(last, s)
        quantize_claims(last, 0)
        expose(last, 3)
        quantize_claims(last, 1)
        for q in last_line:
            aggregate_pass(q, 1)
        for q in range(waiting, JOBS - 2):
            finish(q)
            round_y(q, nc.scalar.copy)
        turn_y(waiting, 2)
        group_y(waiting, 2)
        finish(JOBS - 2)
        finish(JOBS - 1)
        turn_y(waiting + 2, 2)
        group_y(waiting + 2, 2)
        for q in (JOBS - 2, JOBS - 1):
            round_y(q, nc.vector.tensor_copy)
            turn_y(q, 1)
            group_y(q, 1)
        for q0 in (waiting - 4, waiting):
            quantize_y(q0, 2)
            quantize_y(q0 + 2, 2)
            store_words(q0, 4)
        quantize_y(JOBS - 2, 1)
        quantize_y(JOBS - 1, 1)
        store_words(JOBS - 2, 2)
        for quad, queue in enumerate((nc.sync, nc.sync, nc.scalar, nc.scalar)):
            queue.dma_start(
                out=out_2[0, 4 * quad : 4 * quad + 4, :].bitcast(I32),
                in_=plane_scales[32 * quad : 32 * quad + 4, :].bitcast(I32),
            )
